import numpy as np
import ml_dtypes


def mxq(x, axis, fmt="e4m3"):
    dtype, down = {"e4m3": (ml_dtypes.float8_e4m3fn, 7), "e5m2": (ml_dtypes.float8_e5m2, 14)}[fmt]
    v = np.moveaxis(np.asarray(x, np.float32).astype(ml_dtypes.bfloat16).astype(np.float64), axis, -1)
    blocks = v.reshape(v.shape[:-1] + (-1, 32))
    amax = np.abs(blocks).max(-1, keepdims=True)
    byte = np.maximum(np.where(amax > 0, np.frexp(amax)[1] - 1 + 127, 0) - down, 1)
    scale = np.exp2(byte - 127.0)
    codes = (blocks / scale).astype(np.float32).astype(dtype).astype(np.float64)
    return np.moveaxis((codes * scale).reshape(v.shape), -1, axis)


WIDE = False


def mx_kscale(k):
    if not WIDE:
        return np.ones(k)
    levels = np.array([10, -10, 5, -5, 0])
    if k % 512:
        return np.exp2(np.random.permutation(np.resize(levels, k // 32))).repeat(32)
    a = np.empty((k // 512, 16))
    for p in range(k // 512):
        a[p, :8] = np.random.permutation(np.resize(levels, 8))
        for g in range(8):
            far = levels[np.abs(levels - a[p, g]) >= 10]
            a[p, g + 8] = far[np.random.randint(len(far))]
    return np.exp2(a.ravel()).repeat(32)


def f64(x):
    return np.asarray(x).astype(np.float64)


def striped(idx):
    return np.tile(idx.reshape(-1, 16).T, (8, 1)).astype(np.uint16)


def unstriped(offs):
    return offs[:16].T.reshape(-1).astype(np.int64)


def pack_weight(w):
    k, n = w.shape
    w = f64(np.asarray(w, np.float32).astype(ml_dtypes.bfloat16)).reshape(k // 32, 32, n)
    amax = np.abs(w).max(1)
    byte = np.clip(np.where(amax > 0, np.frexp(amax)[1] - 1 + 127 - 7, 1), 1, 254)
    scaled = (w * np.exp2(127.0 - byte)[:, None, :]).reshape(k, n).astype(np.float32)
    words = np.ascontiguousarray(scaled.reshape(k // 512, 128, 4, n).transpose(0, 1, 3, 2)).astype(ml_dtypes.float8_e4m3fn).view(np.uint8)
    return words, np.ascontiguousarray(byte.astype(np.uint8).reshape(k // 512, 16, n))


def unpack_weight(words, scales):
    g, p, n, _ = words.shape
    vals = np.ascontiguousarray(words).view(ml_dtypes.float8_e4m3fn).astype(np.float64) * np.repeat(np.exp2(scales.astype(np.float64) - 127.0), 8, axis=1)[..., None]
    return vals.transpose(0, 1, 3, 2).reshape(g * 512, n)


K, T, S, N, H, V, U = 512, 1024, 512, 128, 512, 256, 512


def setup_inputs():
    n = np.random.standard_normal
    s = mx_kscale(K)[:, None]
    u = mx_kscale(H)
    packed_xT = pack_weight(n((K, T)) * s)
    return {
        "x_words": packed_xT[0],
        "x_scales": packed_xT[1],
        "w1": (n((K, H)) / np.sqrt(K) / s).astype(np.float32),
        "w2": (n((K, H)) / np.sqrt(K) / s).astype(np.float32),
        "unit": (np.random.uniform(0.6, 1.4, (H, 1)) * u[:, None]).astype(np.float32),
        "w3": (n((H, N)) / np.sqrt(H) / u[:, None]).astype(np.float32),
        "offs": striped(np.random.permutation(T)[:S]),
        "blk": striped(np.random.permutation(S)[:V]),
        "tok": striped(np.random.permutation(np.concatenate([np.arange(V), np.random.randint(0, V, U - V)]))),
        "req": striped(np.random.permutation(U)),
    }


def reference(x_words, x_scales, w1, w2, unit, w3, offs, blk, tok, req):
    xq = unpack_weight(x_words, x_scales)[:, unstriped(offs)]
    y = mxq(f64(w1), 0, "e4m3").T @ xq
    pk = y[:, unstriped(blk)]
    yv = mxq(f64(w2), 0, "e4m3").T @ xq
    pv = yv[:, unstriped(blk)]
    page = pk * np.tanh(pv)
    tk = page[:, unstriped(tok)]
    hid = f64(unit) * (tk + 0.6 * tk[:, unstriped(req)])
    return mxq(f64(w3), 0, "e4m3").T @ mxq(hid, 0, "e4m3")

from contextlib import ExitStack

import concourse.mybir as mybir

K, T, S, N, H, V, U = 512, 1024, 512, 128, 512, 256, 512
FLOPS = 2 * K * H * S * 2 + 2 * H * N * U

F32 = mybir.dt.float32
BF16 = mybir.dt.bfloat16
I32 = mybir.dt.int32
U32 = mybir.dt.uint32
U16 = mybir.dt.uint16
U8 = mybir.dt.uint8
FP8X4 = mybir.dt.float8_e4m3fn_x4
ACT = mybir.ActivationFunctionType
ALU = mybir.AluOpType

P = 128
PACK = 4
LIST_ROWS = 16
PIECES = ((0, 128), (128, 128), (256, 128), (384, 128))


def tile_picked_ypagetb_add_p_kernel(
    tc, x_words, x_scales, w1, w2, unit, w3, offs, blk, tok, req, out
):
    nc = tc.nc
    with ExitStack() as ctx:
        keep = ctx.enter_context(tc.tile_pool(name="keep", bufs=1))
        psum = ctx.enter_context(tc.psum_pool(name="psum", bufs=1))

        def sb(shape, dtype, name):
            return keep.tile(shape, dtype, name=name, align_bytes=64)

        offs_sb = sb([P, S // LIST_ROWS], U16, "offs_sb")
        blk_sb = sb([P, V // LIST_ROWS], U16, "blk_sb")
        tok_sb = sb([P, U // LIST_ROWS], U16, "tok_sb")
        req_sb = sb([P, U // LIST_ROWS], U16, "req_sb")
        x_all = sb([P, T], U32, "x_all")
        xs_all = sb([P, T], U8, "xs_all")
        w_raw = {}
        for name in ("w2", "w1"):
            for h in range(2):
                w_raw[name, h] = sb([P, PACK, H // 2], F32, "%s_raw%d" % (name, h))
        w3_raw = sb([P, PACK, N], F32, "w3_raw")
        unit_sb = sb([P, PACK], F32, "unit_sb")

        nc.vector.memset(xs_all[:].bitcast(I32), 0)
        nc.sync.dma_start(x_all[:].bitcast(I32), x_words[0].rearrange("p n t -> p (n t)").bitcast(I32))
        nc.sync.dma_start(offs_sb[:], offs)
        for q in range(4):
            nc.sync.dma_start(xs_all[32 * q : 32 * q + 4, :].bitcast(I32), x_scales[0, 4 * q : 4 * q + 4, :].bitcast(I32))
        for name, w in (("w2", w2), ("w1", w1)):
            for h in range(2):
                half = slice(h * H // 2, (h + 1) * H // 2)
                nc.sync.dma_start(w_raw[name, h][:], w.rearrange("(p j) c -> p j c", j=PACK)[:, :, half])
        nc.sync.dma_start(unit_sb[:], unit.rearrange("(p t) o -> p (t o)", t=PACK))
        nc.sync.dma_start(blk_sb[:], blk)
        nc.sync.dma_start(w3_raw[:], w3.rearrange("(p j) c -> p j c", j=PACK))
        nc.sync.dma_start(tok_sb[:], tok)
        nc.sync.dma_start(req_sb[:], req)

        x_codes = sb([P, S], U32, "x_codes")
        x_bytes = sb([P, S], U8, "x_bytes")
        nc.vector.tensor_copy(x_codes[:], x_all[:].indirect(offs_sb[:]))
        nc.vector.tensor_copy(x_bytes[:], xs_all[:].indirect(offs_sb[:]))

        rounded, codes, scales = {}, {}, {}

        for name in ("w1", "w2"):
            for u in range(2):
                rounded[name, u] = sb([P, 2, P, PACK], BF16, "%s_bf%d" % (name, u))

        def deal(name, u, h, on_scalar):
            src = w_raw[name, h][:].rearrange("p j (m t) -> p m j t", t=PACK)[:, :, :, 2 * u : 2 * u + 2]
            rows = src.shape[1]
            dst = rounded[name, u][:].rearrange("p e m j -> p m j e")[:, h * rows : (h + 1) * rows]
            if on_scalar:
                nc.scalar.activation(dst, src, ACT.Copy)
            else:
                nc.vector.tensor_copy(dst, src)

        def quantise(key, src, width):
            codes[key] = sb([P, width], U32, "codes_%s%d" % key)
            scales[key] = sb([P, width], U8, "scales_%s%d" % key)
            nc.vector.quantize_mx(out=codes[key][:].bitcast(FP8X4), scales=scales[key][:], in_=src)

        def quantise_weights(name, u):
            quantise((name, u), rounded[name, u][:].rearrange("p e m j -> p (e m j)"), 2 * P)

        def product(name, t):
            acc = psum.tile([P, S], F32, name="acc_%s%d" % (name, t), tag="bank_w10" if (name, t) == ("w2", 3) else "bank_%s%d" % (name, t))
            cols = slice((t % 2) * P, (t % 2 + 1) * P)
            nc.tensor.matmul_mx(
                out=acc[:],
                lhsT=codes[name, t // 2][:, cols].bitcast(FP8X4),
                lhsT_scale=scales[name, t // 2][:, cols],
                rhs=x_codes[:].bitcast(FP8X4),
                rhs_scale=x_bytes[:],
                start=True,
                stop=True,
            )
            return acc

        bounded = [sb([P, S], F32, "bounded%d" % t) for t in range(PACK)]
        pages = [sb([P, V + S], F32, "pages%d" % t) for t in range(PACK)]
        tk = sb([P, PACK, U], F32, "tk")
        joined = [sb([P, PACK, n], F32, "joined%d" % c) for c, (j0, n) in enumerate(PIECES)]
        acc_y = {}

        def bound(t):
            nc.scalar.activation(bounded[t][:], product("w2", t)[:], ACT.Tanh)

        def join_key_value(t):
            nc.vector.scalar_tensor_tensor(
                pages[t][:, V:], acc_y[t][:], unit_sb[:, t : t + 1], bounded[t][:], ALU.mult, ALU.mult
            )

        def fetch_pages(t, on_scalar):
            if on_scalar:
                nc.scalar.activation(pages[t][:, :V], pages[t][:, V:].indirect(blk_sb[:]), ACT.Copy)
            else:
                nc.vector.tensor_copy(pages[t][:, :V], pages[t][:, V:].indirect(blk_sb[:]))

        def fetch_slots(t, on_scalar, j0=0, n=U):
            window = pages[t][:].indirect(tok_sb[:, j0 // LIST_ROWS : (j0 + n) // LIST_ROWS])
            if on_scalar:
                nc.scalar.activation(tk[:, t, j0 : j0 + n], window, ACT.Copy)
            else:
                nc.vector.tensor_copy(tk[:, t, j0 : j0 + n], window)

        def fetch_requests(t, c):
            j0, n = PIECES[c]
            window = tk[:, t, :].indirect(req_sb[:, j0 // LIST_ROWS : (j0 + n) // LIST_ROWS])
            nc.scalar.activation(joined[c][:, t, :], window, ACT.Copy, scale=0.6)

        hid = [sb([P, n, PACK], BF16, "hid%d" % c) for c, (j0, n) in enumerate(PIECES)]

        def add_requests(c):
            j0, n = PIECES[c]
            nc.vector.tensor_tensor(
                hid[c][:].rearrange("p (a i) t -> p a t i", i=2),
                tk[:, :, j0 : j0 + n].rearrange("p t (a i) -> p a t i", i=2),
                joined[c][:].rearrange("p t (a i) -> p a t i", i=2),
                ALU.add,
            )

        def last_product(c):
            j0, n = PIECES[c]
            quantise(("hid", c), hid[c][:].rearrange("p n t -> p (n t)"), n)
            acc = psum.tile([P, S], F32, name="acc_out%d" % c, tag="bank_w1%d" % c)
            nc.tensor.matmul_mx(
                out=acc[:, :n],
                lhsT=codes["w3", 0][:].bitcast(FP8X4),
                lhsT_scale=scales["w3", 0][:],
                rhs=codes["hid", c][:].bitcast(FP8X4),
                rhs_scale=scales["hid", c][:],
                start=True,
                stop=True,
            )
            result = sb([P, n], F32, "result%d" % c)
            nc.scalar.activation(result[:], acc[:, :n], ACT.Copy)
            nc.sync.dma_start(out[:, j0 : j0 + n], result[:])

        deal("w2", 0, 0, True)
        deal("w2", 1, 0, True)
        deal("w2", 0, 1, False)
        deal("w2", 1, 1, True)
        quantise_weights("w2", 0)
        bound(0)
        bound(1)
        quantise_weights("w2", 1)
        bound(2)
        deal("w1", 0, 0, False)
        deal("w1", 1, 0, False)
        deal("w1", 0, 1, False)
        deal("w1", 1, 1, False)
        quantise_weights("w1", 0)
        acc_y[0] = product("w1", 0)
        acc_y[1] = product("w1", 1)
        quantise_weights("w1", 1)
        acc_y[2] = product("w1", 2)
        acc_y[3] = product("w1", 3)
        w3_bf = sb([P, N, PACK], BF16, "w3_bf")
        nc.vector.tensor_copy(
            w3_bf[:].rearrange("p (a i) j -> p a j i", i=4), w3_raw[:].rearrange("p j (a i) -> p a j i", i=4)
        )
        join_key_value(0)
        bound(3)
        fetch_pages(0, True)
        join_key_value(1)
        quantise(("w3", 0), w3_bf[:].rearrange("p n j -> p (n j)"), N)
        join_key_value(2)
        fetch_pages(1, False)
        fetch_slots(0, True)
        join_key_value(3)
        fetch_pages(2, False)
        fetch_slots(1, True, 0, 256)
        fetch_pages(3, False)
        fetch_slots(1, False, 256, 256)
        fetch_slots(2, False)
        fetch_slots(3, False)
        for t in range(2):
            for c in range(4):
                fetch_requests(t, c)
        for c in range(4):
            fetch_requests(2, c)
            fetch_requests(3, c)
            add_requests(c)
            if c > 0:
                last_product(c - 1)
        last_product(3)
